import numpy as np
import ml_dtypes


def mxq(x, axis, fmt="e4m3"):
    dtype, down = {"e4m3": (ml_dtypes.float8_e4m3fn, 7), "e5m2": (ml_dtypes.float8_e5m2, 14)}[fmt]
    v = np.moveaxis(np.asarray(x, np.float32).astype(ml_dtypes.bfloat16).astype(np.float64), axis, -1)
    blocks = v.reshape(v.shape[:-1] + (-1, 32))
    amax = np.abs(blocks).max(-1, keepdims=True)
    byte = np.maximum(np.where(amax > 0, np.frexp(amax)[1] - 1 + 127, 0) - down, 1)
    scale = np.exp2(byte - 127.0)
    codes = (blocks / scale).astype(np.float32).astype(dtype).astype(np.float64)
    return np.moveaxis((codes * scale).reshape(v.shape), -1, axis)


WIDE = False


def mx_kscale(k):
    if not WIDE:
        return np.ones(k)
    levels = np.array([10, -10, 5, -5, 0])
    if k % 512:
        return np.exp2(np.random.permutation(np.resize(levels, k // 32))).repeat(32)
    a = np.empty((k // 512, 16))
    for p in range(k // 512):
        a[p, :8] = np.random.permutation(np.resize(levels, 8))
        for g in range(8):
            far = levels[np.abs(levels - a[p, g]) >= 10]
            a[p, g + 8] = far[np.random.randint(len(far))]
    return np.exp2(a.ravel()).repeat(32)


def f64(x):
    return np.asarray(x).astype(np.float64)


def striped8(idx):
    return np.asarray(idx).reshape(8, -1, 16).transpose(0, 2, 1).reshape(128, -1).astype(np.uint16)


def unstriped8(offs):
    return offs.reshape(8, 16, -1).transpose(0, 2, 1).reshape(8, -1).astype(np.int64)


def pick8(x, idx, run):
    r = np.arange(len(x))
    return x[r[:, None], idx[r % (8 * run) // run]]


E2M1 = np.array([0.0, 0.5, 1.0, 1.5, 2.0, 3.0, 4.0, 6.0, -0.0, -0.5, -1.0, -1.5, -2.0, -3.0, -4.0, -6.0])


def pack_weight(w, fmt):
    k, n = w.shape
    w = f64(np.asarray(w, np.float32).astype(ml_dtypes.bfloat16)).reshape(k // 32, 32, n)
    amax = np.abs(w).max(1)
    if fmt == "e4m3":
        byte = np.frexp(amax)[1] - 1 + 127 - 7
    else:
        mant, ex = np.frexp(amax / 6.0)
        byte = np.where(mant > 0.5, ex, ex - 1) + 127
    byte = np.clip(np.where(amax > 0, byte, 1), 1, 254)
    scaled = (w * np.exp2(127.0 - byte)[:, None, :]).reshape(k, n).astype(np.float32)
    by_word = np.ascontiguousarray(scaled.reshape(k // 512, 128, 4, n).transpose(0, 1, 3, 2))
    if fmt == "e4m3":
        words = by_word.astype(ml_dtypes.float8_e4m3fn).view(np.uint8)
    else:
        c = by_word.astype(ml_dtypes.float4_e2m1fn).view(np.uint8) & 0xF
        words = (c[..., 0::2] | (c[..., 1::2] << 4)).reshape(k // 512, 128, 2 * n)
    return np.ascontiguousarray(words), np.ascontiguousarray(byte.astype(np.uint8).reshape(k // 512, 16, n))


def unpack_weight(words, scales, fmt):
    g, _, n = scales.shape
    words = np.ascontiguousarray(words).reshape(g, 128, n, -1)
    if fmt == "e4m3":
        vals = words.view(ml_dtypes.float8_e4m3fn).astype(np.float64)
    else:
        nib = np.empty((g, 128, n, 4), np.uint8)
        nib[..., 0::2] = words & 0xF
        nib[..., 1::2] = words >> 4
        vals = E2M1[nib]
    vals = vals * np.repeat(np.exp2(scales.astype(np.float64) - 127.0), 8, axis=1)[..., None]
    return vals.transpose(0, 1, 3, 2).reshape(g * 512, n)


D, V, Q, I = 512, 2048, 128, 512


def setup_inputs():
    n = np.random.standard_normal
    idx = np.stack([np.random.permutation(V)[:I] for _ in range(8)])
    idx2 = np.stack([np.random.permutation(V)[:I] for _ in range(8)])
    fd = mx_kscale(D)
    vocp = pack_weight(n((D, V)) / fd[:, None], "e4m3")
    return {
        "hid": (n((D, Q)) * 1.0 / np.sqrt(D) * fd[:, None]).astype(np.float32),
        "voc_words": vocp[0],
        "voc_scales": vocp[1],
        "stake": (np.random.uniform(0.5, 2.0, (Q, 1))).astype(np.float32),
        "old": (0.5 * n((Q, V))).astype(np.float32),
        "offs": striped8(idx),
        "offs2": striped8(idx2),
    }


def reference(hid, voc_words, voc_scales, stake, old, offs, offs2):
    idx = unstriped8(offs)
    idx2 = unstriped8(offs2)
    vocu = unpack_weight(voc_words, voc_scales, "e4m3")
    hidq = mxq(f64(hid), 0, "e4m3")
    a = hidq.T @ vocu
    m1 = np.max(a, axis=1, keepdims=True)
    p = np.exp(a - m1)
    z = np.sum(p, axis=1, keepdims=True)
    px = np.exp(pick8(a, idx, 16) - m1)
    px2 = np.exp(pick8(a, idx2, 16) - m1)
    ma = np.sum(px, axis=1, keepdims=True) / z
    mb = np.sum(px2, axis=1, keepdims=True) / z
    dmb = f64(stake) / (ma * mb * 16.0 + 1.0) * 16.0 * ma
    dma = f64(stake) / (ma * mb * 16.0 + 1.0) * 16.0 * mb
    dpx2 = dmb / z
    dpx = dma / z
    dz = dmb * np.sum(px2, axis=1, keepdims=True) / np.square(z) * (-1.0) - dma * np.sum(px, axis=1, keepdims=True) / np.square(z)
    e1 = dpx2 * px2
    s1 = np.zeros((Q, V))
    s1[np.arange(Q)[:, None], idx2[np.arange(Q) % 128 // 16]] = e1
    e2 = dpx * px
    s2 = np.zeros((Q, V))
    s2[np.arange(Q)[:, None], idx[np.arange(Q) % 128 // 16]] = e2
    da = dz * p + s1 + s2
    y = da * 512.0 + f64(old)
    return y

@@ -1,0 +1,183 @@
+from contextlib import ExitStack
+
+import concourse.mybir as mybir
+from concourse.masks import make_identity
+
+D, V, Q, LISTED = 512, 2048, 128, 512
+FLOPS = 2 * D * V * Q
+
+F32 = mybir.dt.float32
+BF16 = mybir.dt.bfloat16
+I32 = mybir.dt.int32
+U32 = mybir.dt.uint32
+U16 = mybir.dt.uint16
+U8 = mybir.dt.uint8
+FP8X4 = mybir.dt.float8_e4m3fn_x4
+ALU = mybir.AluOpType
+ACT = mybir.ActivationFunctionType
+AXIS = mybir.AxisListType
+
+P = 128
+PACK = 4
+BANK = 512
+BANKS = V // BANK
+BLOCKS = BANK // P
+STORE_WIDTHS = (256, 256, 512, 512, 256, 256)
+
+
+def tile_attend_bjointcover_heads_kernel(tc, hid, voc_words, voc_scales, stake, old, offs, offs2, out):
+    nc = tc.nc
+    with ExitStack() as ctx:
+        lists = ctx.enter_context(tc.tile_pool(name="lists", bufs=1))
+        keep = ctx.enter_context(tc.tile_pool(name="keep", bufs=1))
+        psum = ctx.enter_context(tc.psum_pool(name="psum", bufs=1))
+
+        cols = [slice(b * BANK, (b + 1) * BANK) for b in range(BANKS)]
+
+        voc_planes = keep.tile([P, BANK], U8, align_bytes=64)
+        nc.vector.memset(voc_planes[:].bitcast(I32), 0)
+
+        hid_raw = keep.tile([P, PACK, Q], F32)
+        nc.sync.dma_start(out=hid_raw[:], in_=hid.rearrange("(p t) q -> p t q", t=PACK))
+
+        words_hbm = voc_words[0].rearrange("p n t -> p (n t)").bitcast(I32)
+        word_spans = [(0, 1), (1, 2), (2, 4)]
+        word_tiles = [keep.tile([P, (e - s) * BANK], I32, align_bytes=64, name="words%d" % s) for s, e in word_spans]
+        nc.sync.dma_start(out=word_tiles[0][:], in_=words_hbm[:, 0:BANK])
+        for quad in range(4):
+            nc.sync.dma_start(
+                out=voc_planes[32 * quad : 32 * quad + 16, :].bitcast(I32),
+                in_=voc_scales[0, 4 * quad : 4 * quad + 4, :].bitcast(I32).rearrange("f (b n) -> b f n", b=BANKS),
+            )
+        for (s, e), t in list(zip(word_spans, word_tiles))[1:]:
+            nc.sync.dma_start(out=t[:], in_=words_hbm[:, s * BANK : e * BANK])
+        words = []
+        for (s, e), t in zip(word_spans, word_tiles):
+            for b in range(e - s):
+                words.append(t[:, b * BANK : (b + 1) * BANK])
+
+        list1 = lists.tile([P, LISTED // 16], U16, name="list1")
+        list2 = lists.tile([P, LISTED // 16], U16, name="list2")
+        nc.sync.dma_start(list1[:], offs)
+        nc.sync.dma_start(list2[:], offs2)
+        stake_sb = keep.tile([P, 1], F32)
+        nc.sync.dma_start(out=stake_sb[:], in_=stake)
+        old_sb = keep.tile([P, V], F32)
+        nc.sync.dma_start(out=old_sb[:], in_=old)
+
+        ident = keep.tile([P, P], F32)
+        make_identity(nc, ident[:])
+
+        placed1 = keep.tile([P, V], F32)
+        nc.vector.memset(placed1[:], 0.0)
+
+        hid_bf = keep.tile([P, Q, PACK], BF16, align_bytes=64, tag="hid_then_placed2")
+        nc.vector.tensor_copy(out=hid_bf[:], in_=hid_raw[:].rearrange("p t q -> p q t"))
+        hid_codes = keep.tile([P, Q], U32, align_bytes=64)
+        hid_plane = keep.tile([P, Q], U8, align_bytes=64)
+        nc.vector.quantize_mx(out=hid_codes[:].bitcast(FP8X4), scales=hid_plane[:], in_=hid_bf[:].rearrange("p q t -> p (q t)"))
+
+        placed2 = keep.tile([P, V], F32, align_bytes=64, tag="hid_then_placed2")
+        nc.gpsimd.memset(placed2[:], 0.0)
+
+        neg = keep.tile([P, V], F32)
+        neg_max_b = keep.tile([P, BANKS], F32)
+        z_b = keep.tile([P, BANKS], F32)
+        p_b = [keep.tile([P, BANK], F32, name="p%d" % b) for b in range(BANKS)]
+        for b in range(BANKS):
+            scores = psum.tile([P, BANK], F32, name="scores%d" % b, tag="rows%d" % b)
+            nc.tensor.matmul_mx(
+                out=scores[:],
+                lhsT=hid_codes[:].bitcast(FP8X4),
+                lhsT_scale=hid_plane[:],
+                rhs=words[b].bitcast(FP8X4),
+                rhs_scale=voc_planes[4 * b : P, :],
+                start=True,
+                stop=True,
+            )
+            nc.vector.tensor_scalar(neg[:, cols[b]], scores[:], -1.0, None, ALU.mult, ALU.min, accum_out=neg_max_b[:, b : b + 1])
+            nc.scalar.activation(p_b[b][:], neg[:, cols[b]], ACT.Exp, bias=neg_max_b[:, b : b + 1], scale=-1.0, accum_out=z_b[:, b : b + 1])
+
+        neg_max = keep.tile([P, 1], F32)
+        nc.vector.tensor_reduce(neg_max[:], neg_max_b[:], AXIS.X, ALU.min)
+        shift_b = keep.tile([P, BANKS], F32)
+        nc.scalar.activation(shift_b[:], neg_max_b[:], ACT.Exp, bias=neg_max[:], scale=-1.0)
+
+        neg1 = keep.tile([P, LISTED], F32)
+        nc.vector.tensor_copy(neg1[:], neg[:].indirect(list1[:]))
+        neg2 = keep.tile([P, LISTED], F32)
+        nc.vector.tensor_copy(neg2[:], neg[:].indirect(list2[:]))
+        px1 = keep.tile([P, LISTED], F32)
+        sum1 = keep.tile([P, 1], F32)
+        nc.scalar.activation(px1[:], neg1[:], ACT.Exp, bias=neg_max[:], scale=-1.0, accum_out=sum1[:])
+        px2 = keep.tile([P, LISTED], F32)
+        sum2 = keep.tile([P, 1], F32)
+        nc.scalar.activation(px2[:], neg2[:], ACT.Exp, bias=neg_max[:], scale=-1.0, accum_out=sum2[:])
+
+        gain = keep.tile([P, 1], F32)
+        nc.vector.tensor_scalar(gain[:], stake_sb[:], 8192.0, None, ALU.mult)
+        z_parts = keep.tile([P, BANKS], F32)
+        z = keep.tile([P, 1], F32)
+        nc.vector.scalar_tensor_tensor(z_parts[:], shift_b[:], 1.0, z_b[:], ALU.mult, ALU.mult, accum_out=z[:])
+        early = keep.tile([P, BANKS + 1], F32)
+        nc.vector.tensor_tensor(early[:, BANKS : BANKS + 1], sum1[:], gain[:], ALU.mult)
+        sum1_16 = keep.tile([P, 1], F32)
+        nc.vector.tensor_scalar(sum1_16[:], sum1[:], 16.0, None, ALU.mult)
+        z_sq = keep.tile([P, 1], F32)
+        nc.vector.tensor_tensor(z_sq[:], z[:], z[:], ALU.mult)
+        z_inv = keep.tile([P, 1], F32)
+        nc.vector.reciprocal(z_inv[:], z[:])
+        shift_gain = keep.tile([P, BANKS], F32)
+        nc.vector.tensor_scalar(shift_gain[:], shift_b[:], early[:, BANKS : BANKS + 1], -2.0, ALU.mult, ALU.mult)
+
+        denom = keep.tile([P, 1], F32)
+        nc.vector.tensor_scalar(denom[:], sum2[:], sum1_16[:], z_sq[:], ALU.mult, ALU.add)
+        gain2 = keep.tile([P, 1], F32)
+        nc.vector.tensor_tensor(gain2[:], sum2[:], gain[:], ALU.mult)
+        nc.vector.tensor_scalar(early[:, 0:BANKS], shift_gain[:], z_inv[:], sum2[:], ALU.mult, ALU.mult)
+        r = keep.tile([P, 1], F32)
+        nc.vector.reciprocal(r[:], denom[:])
+        e_list1 = keep.tile([P, LISTED], F32)
+        nc.vector.tensor_scalar(e_list1[:], px1[:], r[:], gain2[:], ALU.mult, ALU.mult)
+        coef = keep.tile([P, BANKS + 1], F32)
+        nc.vector.tensor_scalar(coef[:], early[:], r[:], None, ALU.mult)
+        nc.vector.tensor_copy(placed1[:].indirect(list1[:]), e_list1[:])
+
+        e_list2 = keep.tile([P, LISTED], F32)
+        nc.scalar.activation(e_list2[:], px2[:], ACT.Copy, scale=coef[:, BANKS : BANKS + 1])
+        dense_b = [keep.tile([P, BANK], F32, name="dense%d" % b) for b in range(BANKS)]
+        for b in range(BANKS):
+            nc.scalar.activation(dense_b[b][:], p_b[b][:], ACT.Copy, scale=coef[:, b : b + 1])
+        nc.vector.tensor_copy(placed2[:].indirect(list2[:]), e_list2[:])
+
+        turned = [psum.tile([P, BLOCKS, P], F32, name="turned%d" % b, tag="turned%d" % b) for b in range(BANKS)]
+
+        def add_turned(b, term, first, last):
+            for j in range(BLOCKS):
+                nc.tensor.matmul(
+                    turned[b][:, j, :], term[:, j * P : (j + 1) * P], ident[:],
+                    start=first and j == 0, stop=last and j == BLOCKS - 1, is_transpose=True,
+                )
+
+        for b in range(BANKS):
+            add_turned(b, old_sb[:, cols[b]], True, False)
+        for b in range(BANKS):
+            add_turned(b, dense_b[b][:], False, False)
+        rest = []
+        for b in range(BANKS):
+            add_turned(b, placed1[:, cols[b]], False, True)
+        for b in range(BANKS):
+            turned_sb = keep.tile([P, BLOCKS, P], F32, name="turned_sb%d" % b)
+            nc.scalar.copy(turned_sb[:], turned[b][:])
+            back = psum.tile([P, BANK], F32, name="back%d" % b, tag="rows%d" % b)
+            for j in range(BLOCKS):
+                nc.tensor.transpose(back[:, j * P : (j + 1) * P], turned_sb[:, j, :], ident[:])
+            rest.append(back)
+
+        start = 0
+        for i, width in enumerate(STORE_WIDTHS):
+            b, lo = divmod(start, BANK)
+            result = keep.tile([P, width], F32, name="result%d" % i)
+            nc.vector.tensor_tensor(result[:], rest[b][:, lo : lo + width], placed2[:, start : start + width], ALU.add)
+            nc.sync.dma_start(out=out[:, start : start + width], in_=result[:])
+            start = start + width

@@ -115,40 +115,37 @@ def tile_attend_bjointcover_heads_kernel(tc, hid, voc_words, voc_scales, stake, 
         nc.scalar.activation(px2[:], neg2[:], ACT.Exp, bias=neg_max[:], scale=-1.0, accum_out=sum2[:])
 
         gain = keep.tile([P, 1], F32)
-        nc.vector.tensor_scalar(gain[:], stake_sb[:], 8192.0, None, ALU.mult)
+        nc.vector.tensor_scalar(gain[:], stake_sb[:], 512.0, None, ALU.mult)
         z_parts = keep.tile([P, BANKS], F32)
-        z = keep.tile([P, 1], F32)
-        nc.vector.scalar_tensor_tensor(z_parts[:], shift_b[:], 1.0, z_b[:], ALU.mult, ALU.mult, accum_out=z[:])
-        early = keep.tile([P, BANKS + 1], F32)
-        nc.vector.tensor_tensor(early[:, BANKS : BANKS + 1], sum1[:], gain[:], ALU.mult)
-        sum1_16 = keep.tile([P, 1], F32)
-        nc.vector.tensor_scalar(sum1_16[:], sum1[:], 16.0, None, ALU.mult)
+        z_half = keep.tile([P, 1], F32)
+        nc.vector.scalar_tensor_tensor(z_parts[:], shift_b[:], -0.5, z_b[:], ALU.mult, ALU.mult, accum_out=z_half[:])
+        gain1 = keep.tile([P, 1], F32)
+        nc.vector.tensor_tensor(gain1[:], sum1[:], gain[:], ALU.mult)
         z_sq = keep.tile([P, 1], F32)
-        nc.vector.tensor_tensor(z_sq[:], z[:], z[:], ALU.mult)
+        nc.vector.tensor_scalar(z_sq[:], z_half[:], z_half[:], 0.25, ALU.mult, ALU.mult)
         z_inv = keep.tile([P, 1], F32)
-        nc.vector.reciprocal(z_inv[:], z[:])
-        shift_gain = keep.tile([P, BANKS], F32)
-        nc.vector.tensor_scalar(shift_gain[:], shift_b[:], early[:, BANKS : BANKS + 1], -2.0, ALU.mult, ALU.mult)
+        nc.vector.reciprocal(z_inv[:], z_half[:])
+        dense_pre = keep.tile([P, BANKS], F32)
+        nc.vector.tensor_scalar(dense_pre[:], shift_b[:], z_inv[:], sum1[:], ALU.mult, ALU.mult)
 
         denom = keep.tile([P, 1], F32)
-        nc.vector.tensor_scalar(denom[:], sum2[:], sum1_16[:], z_sq[:], ALU.mult, ALU.add)
+        nc.vector.tensor_scalar(denom[:], sum2[:], sum1[:], z_sq[:], ALU.mult, ALU.add)
         gain2 = keep.tile([P, 1], F32)
         nc.vector.tensor_tensor(gain2[:], sum2[:], gain[:], ALU.mult)
-        nc.vector.tensor_scalar(early[:, 0:BANKS], shift_gain[:], z_inv[:], sum2[:], ALU.mult, ALU.mult)
         r = keep.tile([P, 1], F32)
         nc.vector.reciprocal(r[:], denom[:])
         e_list1 = keep.tile([P, LISTED], F32)
         nc.vector.tensor_scalar(e_list1[:], px1[:], r[:], gain2[:], ALU.mult, ALU.mult)
-        coef = keep.tile([P, BANKS + 1], F32)
-        nc.vector.tensor_scalar(coef[:], early[:], r[:], None, ALU.mult)
-        nc.vector.tensor_copy(placed1[:].indirect(list1[:]), e_list1[:])
-
+        coef = keep.tile([P, BANKS], F32)
+        nc.vector.tensor_scalar(coef[:], dense_pre[:], r[:], gain2[:], ALU.mult, ALU.mult)
         e_list2 = keep.tile([P, LISTED], F32)
-        nc.scalar.activation(e_list2[:], px2[:], ACT.Copy, scale=coef[:, BANKS : BANKS + 1])
+        nc.vector.tensor_scalar(e_list2[:], px2[:], r[:], gain1[:], ALU.mult, ALU.mult)
+        nc.vector.tensor_copy(placed1[:].indirect(list1[:]), e_list1[:])
+        nc.vector.tensor_copy(placed2[:].indirect(list2[:]), e_list2[:])
+
         dense_b = [keep.tile([P, BANK], F32, name="dense%d" % b) for b in range(BANKS)]
         for b in range(BANKS):
             nc.scalar.activation(dense_b[b][:], p_b[b][:], ACT.Copy, scale=coef[:, b : b + 1])
-        nc.vector.tensor_copy(placed2[:].indirect(list2[:]), e_list2[:])
 
         turned = [psum.tile([P, BLOCKS, P], F32, name="turned%d" % b, tag="turned%d" % b) for b in range(BANKS)]
 
@@ -159,25 +156,38 @@ def tile_attend_bjointcover_heads_kernel(tc, hid, voc_words, voc_scales, stake, 
                     start=first and j == 0, stop=last and j == BLOCKS - 1, is_transpose=True,
                 )
 
+        turned_sb = keep.tile([P, BANKS * BLOCKS, P], F32)
+
+        def close_turned(b):
+            add_turned(b, placed1[:, cols[b]], False, True)
+            nc.scalar.copy(turned_sb[:, b * BLOCKS : (b + 1) * BLOCKS, :], turned[b][:])
+
+        rest = {}
+
+        def turn_back(first_block, count, tag):
+            bank = psum.tile([P, count * P], F32, name="rest%d" % first_block, tag=tag)
+            for j in range(count):
+                nc.tensor.transpose(bank[:, j * P : (j + 1) * P], turned_sb[:, first_block + j, :], ident[:])
+                rest[first_block + j] = (bank, j * P)
+
         for b in range(BANKS):
             add_turned(b, old_sb[:, cols[b]], True, False)
         for b in range(BANKS):
             add_turned(b, dense_b[b][:], False, False)
-        rest = []
-        for b in range(BANKS):
-            add_turned(b, placed1[:, cols[b]], False, True)
-        for b in range(BANKS):
-            turned_sb = keep.tile([P, BLOCKS, P], F32, name="turned_sb%d" % b)
-            nc.scalar.copy(turned_sb[:], turned[b][:])
-            back = psum.tile([P, BANK], F32, name="back%d" % b, tag="rows%d" % b)
-            for j in range(BLOCKS):
-                nc.tensor.transpose(back[:, j * P : (j + 1) * P], turned_sb[:, j, :], ident[:])
-            rest.append(back)
+        close_turned(0)
+        close_turned(1)
+        close_turned(2)
+        turn_back(0, 4, "rows0")
+        close_turned(3)
+        turn_back(4, 4, "rows1")
+        turn_back(8, 4, "rows2")
+        turn_back(12, 2, "rows3")
+        turn_back(14, 2, "turned0")
 
         start = 0
         for i, width in enumerate(STORE_WIDTHS):
-            b, lo = divmod(start, BANK)
+            bank, lo = rest[start // P]
             result = keep.tile([P, width], F32, name="result%d" % i)
-            nc.vector.tensor_tensor(result[:], rest[b][:, lo : lo + width], placed2[:, start : start + width], ALU.add)
+            nc.vector.tensor_tensor(result[:], bank[:, lo : lo + width], placed2[:, start : start + width], ALU.add)
             nc.sync.dma_start(out=out[:, start : start + width], in_=result[:])
             start = start + width

@@ -22,6 +22,9 @@ PACK = 4
 BANK = 512
 BANKS = V // BANK
 BLOCKS = BANK // P
+SCORE_PIECES = ((0, 256, "rows0"), (256, 512, "turned3"), (512, 1024, "rows1"), (1024, 1536, "rows2"), (1536, 2048, "rows3"))
+PIECES = len(SCORE_PIECES)
+CAST_SPLIT = 88
 STORE_WIDTHS = (256, 256, 512, 512, 256, 256)
 
 
@@ -41,20 +44,15 @@ def tile_attend_bjointcover_heads_kernel(tc, hid, voc_words, voc_scales, stake, 
         nc.sync.dma_start(out=hid_raw[:], in_=hid.rearrange("(p t) q -> p t q", t=PACK))
 
         words_hbm = voc_words[0].rearrange("p n t -> p (n t)").bitcast(I32)
-        word_spans = [(0, 1), (1, 2), (2, 4)]
-        word_tiles = [keep.tile([P, (e - s) * BANK], I32, align_bytes=64, name="words%d" % s) for s, e in word_spans]
-        nc.sync.dma_start(out=word_tiles[0][:], in_=words_hbm[:, 0:BANK])
+        words = [keep.tile([P, BANK], I32, align_bytes=64, name="words%d" % b) for b in range(BANKS)]
+        nc.sync.dma_start(out=words[0][:], in_=words_hbm[:, cols[0]])
         for quad in range(4):
             nc.sync.dma_start(
                 out=voc_planes[32 * quad : 32 * quad + 16, :].bitcast(I32),
                 in_=voc_scales[0, 4 * quad : 4 * quad + 4, :].bitcast(I32).rearrange("f (b n) -> b f n", b=BANKS),
             )
-        for (s, e), t in list(zip(word_spans, word_tiles))[1:]:
-            nc.sync.dma_start(out=t[:], in_=words_hbm[:, s * BANK : e * BANK])
-        words = []
-        for (s, e), t in zip(word_spans, word_tiles):
-            for b in range(e - s):
-                words.append(t[:, b * BANK : (b + 1) * BANK])
+        for b in range(1, BANKS):
+            nc.sync.dma_start(out=words[b][:], in_=words_hbm[:, cols[b]])
 
         list1 = lists.tile([P, LISTED // 16], U16, name="list1")
         list2 = lists.tile([P, LISTED // 16], U16, name="list2")
@@ -69,10 +67,12 @@ def tile_attend_bjointcover_heads_kernel(tc, hid, voc_words, voc_scales, stake, 
         make_identity(nc, ident[:])
 
         placed1 = keep.tile([P, V], F32)
-        nc.vector.memset(placed1[:], 0.0)
+        nc.vector.memset(placed1[:].bitcast(I32), 0)
 
         hid_bf = keep.tile([P, Q, PACK], BF16, align_bytes=64, tag="hid_then_placed2")
-        nc.vector.tensor_copy(out=hid_bf[:], in_=hid_raw[:].rearrange("p t q -> p q t"))
+        hid_turned = hid_raw[:].rearrange("p t q -> p q t")
+        nc.vector.tensor_copy(out=hid_bf[:, 0:CAST_SPLIT, :], in_=hid_turned[:, 0:CAST_SPLIT, :])
+        nc.scalar.copy(hid_bf[:, CAST_SPLIT:Q, :], hid_turned[:, CAST_SPLIT:Q, :])
         hid_codes = keep.tile([P, Q], U32, align_bytes=64)
         hid_plane = keep.tile([P, Q], U8, align_bytes=64)
         nc.vector.quantize_mx(out=hid_codes[:].bitcast(FP8X4), scales=hid_plane[:], in_=hid_bf[:].rearrange("p q t -> p (q t)"))
@@ -81,30 +81,32 @@ def tile_attend_bjointcover_heads_kernel(tc, hid, voc_words, voc_scales, stake, 
         nc.gpsimd.memset(placed2[:], 0.0)
 
         neg = keep.tile([P, V], F32)
-        neg_max_b = keep.tile([P, BANKS], F32)
-        z_b = keep.tile([P, BANKS], F32)
-        p_b = [keep.tile([P, BANK], F32, name="p%d" % b) for b in range(BANKS)]
-        for b in range(BANKS):
-            scores = psum.tile([P, BANK], F32, name="scores%d" % b, tag="rows%d" % b)
+        neg_max_b = keep.tile([P, PIECES], F32)
+        z_b = keep.tile([P, PIECES], F32)
+        p_all = keep.tile([P, V], F32, tag="p_then_ident")
+        for i, (lo, hi, tag) in enumerate(SCORE_PIECES):
+            b = lo // BANK
+            inside = slice(lo - b * BANK, hi - b * BANK)
+            scores = psum.tile([P, hi - lo], F32, name="scores%d" % i, tag=tag)
             nc.tensor.matmul_mx(
                 out=scores[:],
                 lhsT=hid_codes[:].bitcast(FP8X4),
                 lhsT_scale=hid_plane[:],
-                rhs=words[b].bitcast(FP8X4),
-                rhs_scale=voc_planes[4 * b : P, :],
+                rhs=words[b][:, inside].bitcast(FP8X4),
+                rhs_scale=voc_planes[4 * b : P, inside],
                 start=True,
                 stop=True,
             )
-            nc.vector.tensor_scalar(neg[:, cols[b]], scores[:], -1.0, None, ALU.mult, ALU.min, accum_out=neg_max_b[:, b : b + 1])
-            nc.scalar.activation(p_b[b][:], neg[:, cols[b]], ACT.Exp, bias=neg_max_b[:, b : b + 1], scale=-1.0, accum_out=z_b[:, b : b + 1])
-
-        neg_max = keep.tile([P, 1], F32)
-        nc.vector.tensor_reduce(neg_max[:], neg_max_b[:], AXIS.X, ALU.min)
-        shift_b = keep.tile([P, BANKS], F32)
-        nc.scalar.activation(shift_b[:], neg_max_b[:], ACT.Exp, bias=neg_max[:], scale=-1.0)
+            nc.vector.tensor_scalar(neg[:, lo:hi], scores[:], -1.0, None, ALU.mult, ALU.min, accum_out=neg_max_b[:, i : i + 1])
+            nc.scalar.activation(p_all[:, lo:hi], neg[:, lo:hi], ACT.Exp, bias=neg_max_b[:, i : i + 1], scale=-1.0, accum_out=z_b[:, i : i + 1])
 
         neg1 = keep.tile([P, LISTED], F32)
         nc.vector.tensor_copy(neg1[:], neg[:].indirect(list1[:]))
+        neg_max = keep.tile([P, 1], F32)
+        nc.vector.tensor_reduce(neg_max[:], neg_max_b[:], AXIS.X, ALU.min)
+        shift_b = keep.tile([P, PIECES], F32)
+        nc.scalar.activation(shift_b[:], neg_max_b[:], ACT.Exp, bias=neg_max[:], scale=-1.0)
+
         neg2 = keep.tile([P, LISTED], F32)
         nc.vector.tensor_copy(neg2[:], neg[:].indirect(list2[:]))
         px1 = keep.tile([P, LISTED], F32)
@@ -114,29 +116,27 @@ def tile_attend_bjointcover_heads_kernel(tc, hid, voc_words, voc_scales, stake, 
         sum2 = keep.tile([P, 1], F32)
         nc.scalar.activation(px2[:], neg2[:], ACT.Exp, bias=neg_max[:], scale=-1.0, accum_out=sum2[:])
 
-        gain = keep.tile([P, 1], F32)
-        nc.vector.tensor_scalar(gain[:], stake_sb[:], 512.0, None, ALU.mult)
-        z_parts = keep.tile([P, BANKS], F32)
+        z_parts = keep.tile([P, PIECES], F32)
         z_half = keep.tile([P, 1], F32)
         nc.vector.scalar_tensor_tensor(z_parts[:], shift_b[:], -0.5, z_b[:], ALU.mult, ALU.mult, accum_out=z_half[:])
         gain1 = keep.tile([P, 1], F32)
-        nc.vector.tensor_tensor(gain1[:], sum1[:], gain[:], ALU.mult)
+        nc.vector.tensor_scalar(gain1[:], sum1[:], stake_sb[:], 512.0, ALU.mult, ALU.mult)
         z_sq = keep.tile([P, 1], F32)
         nc.vector.tensor_scalar(z_sq[:], z_half[:], z_half[:], 0.25, ALU.mult, ALU.mult)
         z_inv = keep.tile([P, 1], F32)
         nc.vector.reciprocal(z_inv[:], z_half[:])
-        dense_pre = keep.tile([P, BANKS], F32)
+        dense_pre = keep.tile([P, PIECES], F32)
         nc.vector.tensor_scalar(dense_pre[:], shift_b[:], z_inv[:], sum1[:], ALU.mult, ALU.mult)
 
         denom = keep.tile([P, 1], F32)
         nc.vector.tensor_scalar(denom[:], sum2[:], sum1[:], z_sq[:], ALU.mult, ALU.add)
         gain2 = keep.tile([P, 1], F32)
-        nc.vector.tensor_tensor(gain2[:], sum2[:], gain[:], ALU.mult)
+        nc.vector.tensor_scalar(gain2[:], sum2[:], stake_sb[:], 512.0, ALU.mult, ALU.mult)
         r = keep.tile([P, 1], F32)
         nc.vector.reciprocal(r[:], denom[:])
         e_list1 = keep.tile([P, LISTED], F32)
         nc.vector.tensor_scalar(e_list1[:], px1[:], r[:], gain2[:], ALU.mult, ALU.mult)
-        coef = keep.tile([P, BANKS], F32)
+        coef = keep.tile([P, PIECES], F32)
         nc.vector.tensor_scalar(coef[:], dense_pre[:], r[:], gain2[:], ALU.mult, ALU.mult)
         e_list2 = keep.tile([P, LISTED], F32)
         nc.vector.tensor_scalar(e_list2[:], px2[:], r[:], gain1[:], ALU.mult, ALU.mult)
@@ -144,22 +144,26 @@ def tile_attend_bjointcover_heads_kernel(tc, hid, voc_words, voc_scales, stake, 
         nc.vector.tensor_copy(placed2[:].indirect(list2[:]), e_list2[:])
 
         dense_b = [keep.tile([P, BANK], F32, name="dense%d" % b) for b in range(BANKS)]
-        for b in range(BANKS):
-            nc.scalar.activation(dense_b[b][:], p_b[b][:], ACT.Copy, scale=coef[:, b : b + 1])
+        for i, (lo, hi, tag) in enumerate(SCORE_PIECES):
+            b = lo // BANK
+            nc.scalar.activation(dense_b[b][:, lo - b * BANK : hi - b * BANK], p_all[:, lo:hi], ACT.Copy, scale=coef[:, i : i + 1])
+
+        ident_late = keep.tile([P, P], F32, tag="p_then_ident")
+        nc.scalar.copy(ident_late[:], ident[:])
 
         turned = [psum.tile([P, BLOCKS, P], F32, name="turned%d" % b, tag="turned%d" % b) for b in range(BANKS)]
 
-        def add_turned(b, term, first, last):
+        def add_turned(b, term, identity, first, last):
             for j in range(BLOCKS):
                 nc.tensor.matmul(
-                    turned[b][:, j, :], term[:, j * P : (j + 1) * P], ident[:],
+                    turned[b][:, j, :], term[:, j * P : (j + 1) * P], identity[:],
                     start=first and j == 0, stop=last and j == BLOCKS - 1, is_transpose=True,
                 )
 
         turned_sb = keep.tile([P, BANKS * BLOCKS, P], F32)
 
         def close_turned(b):
-            add_turned(b, placed1[:, cols[b]], False, True)
+            add_turned(b, placed1[:, cols[b]], ident_late, False, True)
             nc.scalar.copy(turned_sb[:, b * BLOCKS : (b + 1) * BLOCKS, :], turned[b][:])
 
         rest = {}
@@ -171,9 +175,9 @@ def tile_attend_bjointcover_heads_kernel(tc, hid, voc_words, voc_scales, stake, 
                 rest[first_block + j] = (bank, j * P)
 
         for b in range(BANKS):
-            add_turned(b, old_sb[:, cols[b]], True, False)
+            add_turned(b, old_sb[:, cols[b]], ident, True, False)
         for b in range(BANKS):
-            add_turned(b, dense_b[b][:], False, False)
+            add_turned(b, dense_b[b][:], ident, False, False)
         close_turned(0)
         close_turned(1)
         close_turned(2)

from contextlib import ExitStack

import concourse.mybir as mybir
from concourse.masks import make_identity

D, V, Q, LISTED = 512, 2048, 128, 512
FLOPS = 2 * D * V * Q

F32 = mybir.dt.float32
BF16 = mybir.dt.bfloat16
I32 = mybir.dt.int32
U32 = mybir.dt.uint32
U16 = mybir.dt.uint16
U8 = mybir.dt.uint8
FP8X4 = mybir.dt.float8_e4m3fn_x4
ALU = mybir.AluOpType
ACT = mybir.ActivationFunctionType
AXIS = mybir.AxisListType

P = 128
PACK = 4
BANK = 512
BANKS = V // BANK
BLOCKS = BANK // P
SCORE_PIECES = ((0, 256, "rows0"), (256, 512, "turned3"), (512, 1024, "rows1"), (1024, 1536, "rows2"), (1536, 2048, "rows3"))
PIECES = len(SCORE_PIECES)
CAST_SPLIT = 88
STORE_WIDTHS = (256, 256, 512, 512, 256, 256)


def tile_attend_bjointcover_heads_kernel(tc, hid, voc_words, voc_scales, stake, old, offs, offs2, out):
    nc = tc.nc
    with ExitStack() as ctx:
        lists = ctx.enter_context(tc.tile_pool(name="lists", bufs=1))
        keep = ctx.enter_context(tc.tile_pool(name="keep", bufs=1))
        psum = ctx.enter_context(tc.psum_pool(name="psum", bufs=1))

        cols = [slice(b * BANK, (b + 1) * BANK) for b in range(BANKS)]

        voc_planes = keep.tile([P, BANK], U8, align_bytes=64)
        nc.vector.memset(voc_planes[:].bitcast(I32), 0)

        hid_raw = keep.tile([P, PACK, Q], F32)
        nc.sync.dma_start(out=hid_raw[:], in_=hid.rearrange("(p t) q -> p t q", t=PACK))

        words_hbm = voc_words[0].rearrange("p n t -> p (n t)").bitcast(I32)
        words = [keep.tile([P, BANK], I32, align_bytes=64, name="words%d" % b) for b in range(BANKS)]
        nc.sync.dma_start(out=words[0][:], in_=words_hbm[:, cols[0]])
        for quad in range(4):
            nc.sync.dma_start(
                out=voc_planes[32 * quad : 32 * quad + 16, :].bitcast(I32),
                in_=voc_scales[0, 4 * quad : 4 * quad + 4, :].bitcast(I32).rearrange("f (b n) -> b f n", b=BANKS),
            )
        for b in range(1, BANKS):
            nc.sync.dma_start(out=words[b][:], in_=words_hbm[:, cols[b]])

        list1 = lists.tile([P, LISTED // 16], U16, name="list1")
        list2 = lists.tile([P, LISTED // 16], U16, name="list2")
        nc.sync.dma_start(list1[:], offs)
        nc.sync.dma_start(list2[:], offs2)
        stake_sb = keep.tile([P, 1], F32)
        nc.sync.dma_start(out=stake_sb[:], in_=stake)
        old_sb = keep.tile([P, V], F32)
        nc.sync.dma_start(out=old_sb[:], in_=old)

        ident = keep.tile([P, P], F32)
        make_identity(nc, ident[:])

        placed1 = keep.tile([P, V], F32)
        nc.vector.memset(placed1[:].bitcast(I32), 0)

        hid_bf = keep.tile([P, Q, PACK], BF16, align_bytes=64, tag="hid_then_placed2")
        hid_turned = hid_raw[:].rearrange("p t q -> p q t")
        nc.vector.tensor_copy(out=hid_bf[:, 0:CAST_SPLIT, :], in_=hid_turned[:, 0:CAST_SPLIT, :])
        nc.scalar.copy(hid_bf[:, CAST_SPLIT:Q, :], hid_turned[:, CAST_SPLIT:Q, :])
        hid_codes = keep.tile([P, Q], U32, align_bytes=64)
        hid_plane = keep.tile([P, Q], U8, align_bytes=64)
        nc.vector.quantize_mx(out=hid_codes[:].bitcast(FP8X4), scales=hid_plane[:], in_=hid_bf[:].rearrange("p q t -> p (q t)"))

        placed2 = keep.tile([P, V], F32, align_bytes=64, tag="hid_then_placed2")
        nc.gpsimd.memset(placed2[:], 0.0)

        neg = keep.tile([P, V], F32)
        neg_max_b = keep.tile([P, PIECES], F32)
        z_b = keep.tile([P, PIECES], F32)
        p_all = keep.tile([P, V], F32, tag="p_then_ident")
        for i, (lo, hi, tag) in enumerate(SCORE_PIECES):
            b = lo // BANK
            inside = slice(lo - b * BANK, hi - b * BANK)
            scores = psum.tile([P, hi - lo], F32, name="scores%d" % i, tag=tag)
            nc.tensor.matmul_mx(
                out=scores[:],
                lhsT=hid_codes[:].bitcast(FP8X4),
                lhsT_scale=hid_plane[:],
                rhs=words[b][:, inside].bitcast(FP8X4),
                rhs_scale=voc_planes[4 * b : P, inside],
                start=True,
                stop=True,
            )
            nc.vector.tensor_scalar(neg[:, lo:hi], scores[:], -1.0, None, ALU.mult, ALU.min, accum_out=neg_max_b[:, i : i + 1])
            nc.scalar.activation(p_all[:, lo:hi], neg[:, lo:hi], ACT.Exp, bias=neg_max_b[:, i : i + 1], scale=-1.0, accum_out=z_b[:, i : i + 1])

        neg1 = keep.tile([P, LISTED], F32)
        nc.vector.tensor_copy(neg1[:], neg[:].indirect(list1[:]))
        neg_max = keep.tile([P, 1], F32)
        nc.vector.tensor_reduce(neg_max[:], neg_max_b[:], AXIS.X, ALU.min)
        shift_b = keep.tile([P, PIECES], F32)
        nc.scalar.activation(shift_b[:], neg_max_b[:], ACT.Exp, bias=neg_max[:], scale=-1.0)

        neg2 = keep.tile([P, LISTED], F32)
        nc.vector.tensor_copy(neg2[:], neg[:].indirect(list2[:]))
        px1 = keep.tile([P, LISTED], F32)
        sum1 = keep.tile([P, 1], F32)
        nc.scalar.activation(px1[:], neg1[:], ACT.Exp, bias=neg_max[:], scale=-1.0, accum_out=sum1[:])
        px2 = keep.tile([P, LISTED], F32)
        sum2 = keep.tile([P, 1], F32)
        nc.scalar.activation(px2[:], neg2[:], ACT.Exp, bias=neg_max[:], scale=-1.0, accum_out=sum2[:])

        z_parts = keep.tile([P, PIECES], F32)
        z_half = keep.tile([P, 1], F32)
        nc.vector.scalar_tensor_tensor(z_parts[:], shift_b[:], -0.5, z_b[:], ALU.mult, ALU.mult, accum_out=z_half[:])
        gain1 = keep.tile([P, 1], F32)
        nc.vector.tensor_scalar(gain1[:], sum1[:], stake_sb[:], 512.0, ALU.mult, ALU.mult)
        z_sq = keep.tile([P, 1], F32)
        nc.vector.tensor_scalar(z_sq[:], z_half[:], z_half[:], 0.25, ALU.mult, ALU.mult)
        z_inv = keep.tile([P, 1], F32)
        nc.vector.reciprocal(z_inv[:], z_half[:])
        dense_pre = keep.tile([P, PIECES], F32)
        nc.vector.tensor_scalar(dense_pre[:], shift_b[:], z_inv[:], sum1[:], ALU.mult, ALU.mult)

        denom = keep.tile([P, 1], F32)
        nc.vector.tensor_scalar(denom[:], sum2[:], sum1[:], z_sq[:], ALU.mult, ALU.add)
        gain2 = keep.tile([P, 1], F32)
        nc.vector.tensor_scalar(gain2[:], sum2[:], stake_sb[:], 512.0, ALU.mult, ALU.mult)
        r = keep.tile([P, 1], F32)
        nc.vector.reciprocal(r[:], denom[:])
        e_list1 = keep.tile([P, LISTED], F32)
        nc.vector.tensor_scalar(e_list1[:], px1[:], r[:], gain2[:], ALU.mult, ALU.mult)
        coef = keep.tile([P, PIECES], F32)
        nc.vector.tensor_scalar(coef[:], dense_pre[:], r[:], gain2[:], ALU.mult, ALU.mult)
        e_list2 = keep.tile([P, LISTED], F32)
        nc.vector.tensor_scalar(e_list2[:], px2[:], r[:], gain1[:], ALU.mult, ALU.mult)
        nc.vector.tensor_copy(placed1[:].indirect(list1[:]), e_list1[:])
        nc.vector.tensor_copy(placed2[:].indirect(list2[:]), e_list2[:])

        dense_b = [keep.tile([P, BANK], F32, name="dense%d" % b) for b in range(BANKS)]
        for i, (lo, hi, tag) in enumerate(SCORE_PIECES):
            b = lo // BANK
            nc.scalar.activation(dense_b[b][:, lo - b * BANK : hi - b * BANK], p_all[:, lo:hi], ACT.Copy, scale=coef[:, i : i + 1])

        ident_late = keep.tile([P, P], F32, tag="p_then_ident")
        nc.scalar.copy(ident_late[:], ident[:])

        turned = [psum.tile([P, BLOCKS, P], F32, name="turned%d" % b, tag="turned%d" % b) for b in range(BANKS)]

        def add_turned(b, term, identity, first, last):
            for j in range(BLOCKS):
                nc.tensor.matmul(
                    turned[b][:, j, :], term[:, j * P : (j + 1) * P], identity[:],
                    start=first and j == 0, stop=last and j == BLOCKS - 1, is_transpose=True,
                )

        turned_sb = keep.tile([P, BANKS * BLOCKS, P], F32)

        def close_turned(b):
            add_turned(b, placed1[:, cols[b]], ident_late, False, True)
            nc.scalar.copy(turned_sb[:, b * BLOCKS : (b + 1) * BLOCKS, :], turned[b][:])

        rest = {}

        def turn_back(first_block, count, tag):
            bank = psum.tile([P, count * P], F32, name="rest%d" % first_block, tag=tag)
            for j in range(count):
                nc.tensor.transpose(bank[:, j * P : (j + 1) * P], turned_sb[:, first_block + j, :], ident[:])
                rest[first_block + j] = (bank, j * P)

        for b in range(BANKS):
            add_turned(b, old_sb[:, cols[b]], ident, True, False)
        for b in range(BANKS):
            add_turned(b, dense_b[b][:], ident, False, False)
        close_turned(0)
        close_turned(1)
        close_turned(2)
        turn_back(0, 4, "rows0")
        close_turned(3)
        turn_back(4, 4, "rows1")
        turn_back(8, 4, "rows2")
        turn_back(12, 2, "rows3")
        turn_back(14, 2, "turned0")

        start = 0
        for i, width in enumerate(STORE_WIDTHS):
            bank, lo = rest[start // P]
            result = keep.tile([P, width], F32, name="result%d" % i)
            nc.vector.tensor_tensor(result[:], bank[:, lo : lo + width], placed2[:, start : start + width], ALU.add)
            nc.sync.dma_start(out=out[:, start : start + width], in_=result[:])
            start = start + width
